import numpy as np
import ml_dtypes


def mxq(x, axis, fmt="e4m3"):
    dtype, down = {"e4m3": (ml_dtypes.float8_e4m3fn, 7), "e5m2": (ml_dtypes.float8_e5m2, 14)}[fmt]
    v = np.moveaxis(np.asarray(x, np.float32).astype(ml_dtypes.bfloat16).astype(np.float64), axis, -1)
    blocks = v.reshape(v.shape[:-1] + (-1, 32))
    amax = np.abs(blocks).max(-1, keepdims=True)
    byte = np.maximum(np.where(amax > 0, np.frexp(amax)[1] - 1 + 127, 0) - down, 1)
    scale = np.exp2(byte - 127.0)
    codes = (blocks / scale).astype(np.float32).astype(dtype).astype(np.float64)
    return np.moveaxis((codes * scale).reshape(v.shape), -1, axis)


WIDE = False


def mx_kscale(k):
    if not WIDE:
        return np.ones(k)
    levels = np.array([10, -10, 5, -5, 0])
    if k % 512:
        return np.exp2(np.random.permutation(np.resize(levels, k // 32))).repeat(32)
    a = np.empty((k // 512, 16))
    for p in range(k // 512):
        a[p, :8] = np.random.permutation(np.resize(levels, 8))
        for g in range(8):
            far = levels[np.abs(levels - a[p, g]) >= 10]
            a[p, g + 8] = far[np.random.randint(len(far))]
    return np.exp2(a.ravel()).repeat(32)


def f64(x):
    return np.asarray(x).astype(np.float64)


def striped(idx):
    return np.tile(idx.reshape(-1, 16).T, (8, 1)).astype(np.uint16)


def unstriped(offs):
    return offs[:16].T.reshape(-1).astype(np.int64)


E2M1 = np.array([0.0, 0.5, 1.0, 1.5, 2.0, 3.0, 4.0, 6.0, -0.0, -0.5, -1.0, -1.5, -2.0, -3.0, -4.0, -6.0])


def pack_weight(w, fmt):
    k, n = w.shape
    w = f64(np.asarray(w, np.float32).astype(ml_dtypes.bfloat16)).reshape(k // 32, 32, n)
    amax = np.abs(w).max(1)
    if fmt == "e4m3":
        byte = np.frexp(amax)[1] - 1 + 127 - 7
    else:
        mant, ex = np.frexp(amax / 6.0)
        byte = np.where(mant > 0.5, ex, ex - 1) + 127
    byte = np.clip(np.where(amax > 0, byte, 1), 1, 254)
    scaled = (w * np.exp2(127.0 - byte)[:, None, :]).reshape(k, n).astype(np.float32)
    by_word = np.ascontiguousarray(scaled.reshape(k // 512, 128, 4, n).transpose(0, 1, 3, 2))
    if fmt == "e4m3":
        words = by_word.astype(ml_dtypes.float8_e4m3fn).view(np.uint8)
    else:
        c = by_word.astype(ml_dtypes.float4_e2m1fn).view(np.uint8) & 0xF
        words = (c[..., 0::2] | (c[..., 1::2] << 4)).reshape(k // 512, 128, 2 * n)
    return np.ascontiguousarray(words), np.ascontiguousarray(byte.astype(np.uint8).reshape(k // 512, 16, n))


def unpack_weight(words, scales, fmt):
    g, _, n = scales.shape
    words = np.ascontiguousarray(words).reshape(g, 128, n, -1)
    if fmt == "e4m3":
        vals = words.view(ml_dtypes.float8_e4m3fn).astype(np.float64)
    else:
        nib = np.empty((g, 128, n, 4), np.uint8)
        nib[..., 0::2] = words & 0xF
        nib[..., 1::2] = words >> 4
        vals = E2M1[nib]
    vals = vals * np.repeat(np.exp2(scales.astype(np.float64) - 127.0), 8, axis=1)[..., None]
    return vals.transpose(0, 1, 3, 2).reshape(g * 512, n)


K, T, E, C, N = 1024, 1024, 6, 128, 384
K8 = 512


def by_expert(wq, xq):
    return np.concatenate([wq[e].T @ xq[:, e * C:(e + 1) * C] for e in range(E)], axis=1)


def setup_inputs():
    n = np.random.standard_normal
    s = mx_kscale(K)[:, None]
    w = n((E, K, N)) / np.sqrt(K) / s[None]
    w8 = [pack_weight(m[:K8], "e4m3") for m in w]
    w4 = [pack_weight(m[K8:], "e2m1") for m in w]
    return {
        "xT": (n((K, T)) * s).astype(np.float32),
        "w8_words": np.stack([m[0] for m in w8]),
        "w8_scales": np.stack([m[1] for m in w8]),
        "w4_words": np.stack([m[0] for m in w4]),
        "w4_scales": np.stack([m[1] for m in w4]),
        "gate": np.tile(np.random.uniform(0.2, 1.0, E * C), (N, 1)).astype(np.float32),
        "offs": striped(np.random.permutation(T)[:E * C]),
    }


def reference(xT, w8_words, w8_scales, w4_words, w4_scales, gate, offs):
    idx = unstriped(offs)
    w = np.stack([np.concatenate([unpack_weight(w8_words[e], w8_scales[e], "e4m3"), unpack_weight(w4_words[e], w4_scales[e], "e2m1")]) for e in range(E)])
    xq = mxq(f64(xT)[:, idx], 0, "e4m3")
    y = by_expert(w, xq)
    out = np.zeros((N, T))
    out[:, idx] = f64(gate) * y
    return out

@@ -1,0 +1,175 @@
+from contextlib import ExitStack
+
+import concourse.mybir as mybir
+
+F32 = mybir.dt.float32
+BF16 = mybir.dt.bfloat16
+I32 = mybir.dt.int32
+U32 = mybir.dt.uint32
+U16 = mybir.dt.uint16
+U8 = mybir.dt.uint8
+FP8X4 = mybir.dt.float8_e4m3fn_x4
+FP4X4 = mybir.dt.float4_e2m1fn_x4
+MULT = mybir.AluOpType.mult
+
+P = 128
+PACK = 4
+K_PASS = P * PACK
+K, T, E, C, N = 1024, 1024, 6, 128, 384
+S = E * C
+N_BLOCKS = N // P
+PASSES = K // K_PASS
+RUNS = [(0, 2), (2, 6)]
+ROWS = [4, 0]
+
+FLOPS = 2 * S * K * N
+BYTES = 4 * K * T + E * N * (4 * P + 2 * P + 2 * 16) + 4 * S + 2 * S + 4 * N * T
+
+CHUNKS = [(0, 0, 512, 320), (0, 512, 512, 320), (1, 0, 512, 384), (1, 512, 256, 128), (1, 768, 256, 80)]
+
+
+def tile_moe_pln_lin_none_kernel(tc, xT, w8_words, w8_scales, w4_words, w4_scales, gate, offs, out):
+    nc = tc.nc
+    with ExitStack() as ctx:
+        keep = ctx.enter_context(tc.tile_pool(name="keep", bufs=1))
+        psum = ctx.enter_context(tc.psum_pool(name="psum", bufs=1))
+
+        offsets = keep.tile([P, S // 16], U16, name="offsets")
+
+        raws = []
+        groups = []
+        for i, (a, t0, width, unused) in enumerate(CHUNKS):
+            raws.append(keep.tile([P, PACK, width], F32, name="raw%d" % i))
+            groups.append(keep.tile([P, width, PACK], BF16, name="grouped%d" % i, align_bytes=64))
+
+        def load_tokens(i):
+            a, t0, width, unused = CHUNKS[i]
+            rows = xT[a * K_PASS : (a + 1) * K_PASS, t0 : t0 + width]
+            nc.sync.dma_start(out=raws[i][:], in_=rows.rearrange("(p j) t -> p j t", j=PACK))
+
+        load_tokens(0)
+        load_tokens(1)
+        nc.sync.dma_start(offsets[:], offs)
+        for i in range(2, len(CHUNKS)):
+            load_tokens(i)
+
+        token_words, slot_words = [], []
+        for a in range(PASSES):
+            token_words.append(keep.tile([P, T], U32, name="token_words%d" % a, align_bytes=64))
+            slot_words.append(keep.tile([P, S], U32, name="slot_words%d" % a, align_bytes=64))
+        token_bytes = keep.tile([P, T], U8, name="token_bytes", align_bytes=64)
+        slot_bytes = keep.tile([P, S], U8, name="slot_bytes", align_bytes=64)
+        nc.gpsimd.memset(token_bytes[:].bitcast(I32), 0)
+
+        w8 = keep.tile([P, E, 4 * N], U8, name="w8", align_bytes=64)
+        w4 = keep.tile([P, E, 2 * N], U8, name="w4", align_bytes=64)
+        w8_plane = keep.tile([P, E, N], U8, name="w8_plane", align_bytes=64)
+        w4_plane = keep.tile([P, E, N], U8, name="w4_plane", align_bytes=64)
+        for plane in (w8_plane, w4_plane):
+            nc.gpsimd.memset(plane[:].rearrange("p e n -> p (e n)").bitcast(I32), 0)
+
+        windows = []
+        for m in range(N_BLOCKS):
+            windows.append(keep.tile([P, T], F32, name="window%d" % m))
+            nc.vector.memset(windows[m][:], 0.0)
+
+        gates = keep.tile([P, S], F32, name="gates")
+
+        def load_scales(plane, scales, row):
+            for q in range(4):
+                nc.sync.dma_start(
+                    out=plane[32 * q + row : 32 * q + row + 4, :, :].bitcast(I32),
+                    in_=scales[:, 0, 4 * q : 4 * q + 4, :].rearrange("e q n -> q e n").bitcast(I32),
+                )
+
+        def load_w8(run):
+            es = slice(run[0], run[1])
+            nc.sync.dma_start(out=w8[:, es, :].bitcast(I32), in_=w8_words[es, 0].rearrange("e p n r -> p e (n r)").bitcast(I32))
+
+        def load_w4(run):
+            es = slice(run[0], run[1])
+            nc.sync.dma_start(out=w4[:, es, :].bitcast(I32), in_=w4_words[es, 0].rearrange("e p b -> p e b").bitcast(I32))
+
+        load_scales(w8_plane, w8_scales, ROWS[0])
+        load_w8(RUNS[0])
+        load_scales(w4_plane, w4_scales, ROWS[1])
+        load_w4(RUNS[0])
+        nc.sync.dma_start(out=gates[:], in_=gate[0:P, :])
+        load_w8(RUNS[1])
+        load_w4(RUNS[1])
+
+        def interleave(i):
+            width, share = CHUNKS[i][2:]
+            for engine, cols in ((nc.scalar.copy, slice(0, share)), (nc.vector.tensor_copy, slice(share, width))):
+                engine(out=groups[i][:, cols, :], in_=raws[i][:, :, cols].rearrange("p j t -> p t j"))
+
+        def quantise(i):
+            a, t0, width, unused = CHUNKS[i]
+            nc.vector.quantize_mx(
+                out=token_words[a][:, t0 : t0 + width].bitcast(FP8X4),
+                scales=token_bytes[ROWS[a] :, t0 : t0 + width],
+                in_=groups[i][:].rearrange("p t j -> p (t j)"),
+            )
+
+        def gather(tokens, slots, s0, s1):
+            nc.vector.tensor_copy(slots[:, s0:s1], tokens[:].indirect(offsets[:, s0 // 16 : s1 // 16]))
+
+        interleave(0)
+        quantise(0)
+        interleave(1)
+        quantise(1)
+        gather(token_words[0], slot_words[0], 0, S)
+        interleave(2)
+        interleave(3)
+        quantise(2)
+        quantise(3)
+        interleave(4)
+        quantise(4)
+        for e0, e1 in RUNS:
+            gather(token_words[1], slot_words[1], e0 * C, e1 * C)
+            gather(token_bytes, slot_bytes, e0 * C, e1 * C)
+
+        results = []
+        for m in range(N_BLOCKS):
+            results.append(keep.tile([P, S], F32, name="result%d" % m))
+
+        def multiply(run, m):
+            e0, e1 = run
+            acc = psum.tile([P, (e1 - e0) * C], F32, name="acc%d_%d" % (e0, m))
+            for e in range(e0, e1):
+                i = e - e0
+                cols = slice(e * C, (e + 1) * C)
+                for a in range(PASSES):
+                    if a == 0:
+                        codes = w8[:, e, 4 * P * m : 4 * P * (m + 1)].bitcast(FP8X4)
+                        plane = w8_plane
+                    else:
+                        codes = w4[:, e, 2 * P * m : 2 * P * (m + 1)].bitcast(FP4X4)
+                        plane = w4_plane
+                    nc.tensor.matmul_mx(
+                        out=acc[:, i * C : (i + 1) * C],
+                        lhsT=codes,
+                        lhsT_scale=plane[ROWS[a] :, e, P * m : P * (m + 1)],
+                        rhs=slot_words[a][:, cols].bitcast(FP8X4),
+                        rhs_scale=slot_bytes[ROWS[a] :, cols],
+                        start=(a == 0),
+                        stop=(a == PASSES - 1),
+                    )
+            nc.scalar.copy(out=results[m][:, e0 * C : e1 * C], in_=acc[:])
+
+        for run in RUNS:
+            for m in range(N_BLOCKS):
+                multiply(run, m)
+
+        def scatter(m, s0, s1):
+            nc.vector.tensor_tensor(
+                windows[m][:].indirect(offsets[:, s0 // 16 : s1 // 16]),
+                results[m][:, s0:s1],
+                gates[:, s0:s1],
+                MULT,
+            )
+
+        for m in range(N_BLOCKS):
+            for e0, e1 in RUNS if m == 0 else [(0, E)]:
+                scatter(m, e0 * C, e1 * C)
+            nc.sync.dma_start(out=out[m * P : (m + 1) * P, :], in_=windows[m][:])

@@ -25,7 +25,7 @@ ROWS = [4, 0]
 FLOPS = 2 * S * K * N
 BYTES = 4 * K * T + E * N * (4 * P + 2 * P + 2 * 16) + 4 * S + 2 * S + 4 * N * T
 
-CHUNKS = [(0, 0, 512, 320), (0, 512, 512, 320), (1, 0, 512, 384), (1, 512, 256, 128), (1, 768, 256, 80)]
+CHUNKS = [(0, 0, 512, 192), (0, 512, 512, 192), (1, 0, 512, 320), (1, 512, 256, 256), (1, 768, 256, 96)]
 
 
 def tile_moe_pln_lin_none_kernel(tc, xT, w8_words, w8_scales, w4_words, w4_scales, gate, offs, out):
@@ -101,7 +101,12 @@ def tile_moe_pln_lin_none_kernel(tc, xT, w8_words, w8_scales, w4_words, w4_scale
         def interleave(i):
             width, share = CHUNKS[i][2:]
             for engine, cols in ((nc.scalar.copy, slice(0, share)), (nc.vector.tensor_copy, slice(share, width))):
-                engine(out=groups[i][:, cols, :], in_=raws[i][:, :, cols].rearrange("p j t -> p t j"))
+                if cols.start == cols.stop:
+                    continue
+                engine(
+                    out=groups[i][:, cols, :].rearrange("p (c i) j -> p c j i", i=4),
+                    in_=raws[i][:, :, cols].rearrange("p j (c i) -> p c j i", i=4),
+                )
 
         def quantise(i):
             a, t0, width, unused = CHUNKS[i]
@@ -122,8 +127,8 @@ def tile_moe_pln_lin_none_kernel(tc, xT, w8_words, w8_scales, w4_words, w4_scale
         interleave(2)
         interleave(3)
         quantise(2)
-        quantise(3)
         interleave(4)
+        quantise(3)
         quantise(4)
         for e0, e1 in RUNS:
             gather(token_words[1], slot_words[1], e0 * C, e1 * C)
@@ -169,7 +174,8 @@ def tile_moe_pln_lin_none_kernel(tc, xT, w8_words, w8_scales, w4_words, w4_scale
                 MULT,
             )
 
-        for m in range(N_BLOCKS):
-            for e0, e1 in RUNS if m == 0 else [(0, E)]:
+        for e0, e1 in RUNS:
+            for m in range(N_BLOCKS):
                 scatter(m, e0 * C, e1 * C)
+        for m in range(N_BLOCKS):
             nc.sync.dma_start(out=out[m * P : (m + 1) * P, :], in_=windows[m][:])

from contextlib import ExitStack

import concourse.mybir as mybir

F32 = mybir.dt.float32
BF16 = mybir.dt.bfloat16
I32 = mybir.dt.int32
U32 = mybir.dt.uint32
U16 = mybir.dt.uint16
U8 = mybir.dt.uint8
FP8X4 = mybir.dt.float8_e4m3fn_x4
FP4X4 = mybir.dt.float4_e2m1fn_x4
MULT = mybir.AluOpType.mult

P = 128
PACK = 4
K_PASS = P * PACK
K, T, E, C, N = 1024, 1024, 6, 128, 384
S = E * C
N_BLOCKS = N // P
PASSES = K // K_PASS
RUNS = [(0, 2), (2, 6)]
ROWS = [4, 0]

FLOPS = 2 * S * K * N
BYTES = 4 * K * T + E * N * (4 * P + 2 * P + 2 * 16) + 4 * S + 2 * S + 4 * N * T

CHUNKS = [(0, 0, 512, 192), (0, 512, 512, 192), (1, 0, 512, 320), (1, 512, 256, 256), (1, 768, 256, 96)]


def tile_moe_pln_lin_none_kernel(tc, xT, w8_words, w8_scales, w4_words, w4_scales, gate, offs, out):
    nc = tc.nc
    with ExitStack() as ctx:
        keep = ctx.enter_context(tc.tile_pool(name="keep", bufs=1))
        psum = ctx.enter_context(tc.psum_pool(name="psum", bufs=1))

        offsets = keep.tile([P, S // 16], U16, name="offsets")

        raws = []
        groups = []
        for i, (a, t0, width, unused) in enumerate(CHUNKS):
            raws.append(keep.tile([P, PACK, width], F32, name="raw%d" % i))
            groups.append(keep.tile([P, width, PACK], BF16, name="grouped%d" % i, align_bytes=64))

        def load_tokens(i):
            a, t0, width, unused = CHUNKS[i]
            rows = xT[a * K_PASS : (a + 1) * K_PASS, t0 : t0 + width]
            nc.sync.dma_start(out=raws[i][:], in_=rows.rearrange("(p j) t -> p j t", j=PACK))

        load_tokens(0)
        load_tokens(1)
        nc.sync.dma_start(offsets[:], offs)
        for i in range(2, len(CHUNKS)):
            load_tokens(i)

        token_words, slot_words = [], []
        for a in range(PASSES):
            token_words.append(keep.tile([P, T], U32, name="token_words%d" % a, align_bytes=64))
            slot_words.append(keep.tile([P, S], U32, name="slot_words%d" % a, align_bytes=64))
        token_bytes = keep.tile([P, T], U8, name="token_bytes", align_bytes=64)
        slot_bytes = keep.tile([P, S], U8, name="slot_bytes", align_bytes=64)
        nc.gpsimd.memset(token_bytes[:].bitcast(I32), 0)

        w8 = keep.tile([P, E, 4 * N], U8, name="w8", align_bytes=64)
        w4 = keep.tile([P, E, 2 * N], U8, name="w4", align_bytes=64)
        w8_plane = keep.tile([P, E, N], U8, name="w8_plane", align_bytes=64)
        w4_plane = keep.tile([P, E, N], U8, name="w4_plane", align_bytes=64)
        for plane in (w8_plane, w4_plane):
            nc.gpsimd.memset(plane[:].rearrange("p e n -> p (e n)").bitcast(I32), 0)

        windows = []
        for m in range(N_BLOCKS):
            windows.append(keep.tile([P, T], F32, name="window%d" % m))
            nc.vector.memset(windows[m][:], 0.0)

        gates = keep.tile([P, S], F32, name="gates")

        def load_scales(plane, scales, row):
            for q in range(4):
                nc.sync.dma_start(
                    out=plane[32 * q + row : 32 * q + row + 4, :, :].bitcast(I32),
                    in_=scales[:, 0, 4 * q : 4 * q + 4, :].rearrange("e q n -> q e n").bitcast(I32),
                )

        def load_w8(run):
            es = slice(run[0], run[1])
            nc.sync.dma_start(out=w8[:, es, :].bitcast(I32), in_=w8_words[es, 0].rearrange("e p n r -> p e (n r)").bitcast(I32))

        def load_w4(run):
            es = slice(run[0], run[1])
            nc.sync.dma_start(out=w4[:, es, :].bitcast(I32), in_=w4_words[es, 0].rearrange("e p b -> p e b").bitcast(I32))

        load_scales(w8_plane, w8_scales, ROWS[0])
        load_w8(RUNS[0])
        load_scales(w4_plane, w4_scales, ROWS[1])
        load_w4(RUNS[0])
        nc.sync.dma_start(out=gates[:], in_=gate[0:P, :])
        load_w8(RUNS[1])
        load_w4(RUNS[1])

        def interleave(i):
            width, share = CHUNKS[i][2:]
            for engine, cols in ((nc.scalar.copy, slice(0, share)), (nc.vector.tensor_copy, slice(share, width))):
                if cols.start == cols.stop:
                    continue
                engine(
                    out=groups[i][:, cols, :].rearrange("p (c i) j -> p c j i", i=4),
                    in_=raws[i][:, :, cols].rearrange("p j (c i) -> p c j i", i=4),
                )

        def quantise(i):
            a, t0, width, unused = CHUNKS[i]
            nc.vector.quantize_mx(
                out=token_words[a][:, t0 : t0 + width].bitcast(FP8X4),
                scales=token_bytes[ROWS[a] :, t0 : t0 + width],
                in_=groups[i][:].rearrange("p t j -> p (t j)"),
            )

        def gather(tokens, slots, s0, s1):
            nc.vector.tensor_copy(slots[:, s0:s1], tokens[:].indirect(offsets[:, s0 // 16 : s1 // 16]))

        interleave(0)
        quantise(0)
        interleave(1)
        quantise(1)
        gather(token_words[0], slot_words[0], 0, S)
        interleave(2)
        interleave(3)
        quantise(2)
        interleave(4)
        quantise(3)
        quantise(4)
        for e0, e1 in RUNS:
            gather(token_words[1], slot_words[1], e0 * C, e1 * C)
            gather(token_bytes, slot_bytes, e0 * C, e1 * C)

        results = []
        for m in range(N_BLOCKS):
            results.append(keep.tile([P, S], F32, name="result%d" % m))

        def multiply(run, m):
            e0, e1 = run
            acc = psum.tile([P, (e1 - e0) * C], F32, name="acc%d_%d" % (e0, m))
            for e in range(e0, e1):
                i = e - e0
                cols = slice(e * C, (e + 1) * C)
                for a in range(PASSES):
                    if a == 0:
                        codes = w8[:, e, 4 * P * m : 4 * P * (m + 1)].bitcast(FP8X4)
                        plane = w8_plane
                    else:
                        codes = w4[:, e, 2 * P * m : 2 * P * (m + 1)].bitcast(FP4X4)
                        plane = w4_plane
                    nc.tensor.matmul_mx(
                        out=acc[:, i * C : (i + 1) * C],
                        lhsT=codes,
                        lhsT_scale=plane[ROWS[a] :, e, P * m : P * (m + 1)],
                        rhs=slot_words[a][:, cols].bitcast(FP8X4),
                        rhs_scale=slot_bytes[ROWS[a] :, cols],
                        start=(a == 0),
                        stop=(a == PASSES - 1),
                    )
            nc.scalar.copy(out=results[m][:, e0 * C : e1 * C], in_=acc[:])

        for run in RUNS:
            for m in range(N_BLOCKS):
                multiply(run, m)

        def scatter(m, s0, s1):
            nc.vector.tensor_tensor(
                windows[m][:].indirect(offsets[:, s0 // 16 : s1 // 16]),
                results[m][:, s0:s1],
                gates[:, s0:s1],
                MULT,
            )

        for e0, e1 in RUNS:
            for m in range(N_BLOCKS):
                scatter(m, e0 * C, e1 * C)
        for m in range(N_BLOCKS):
            nc.sync.dma_start(out=out[m * P : (m + 1) * P, :], in_=windows[m][:])
